import numpy as np
import ml_dtypes


def mxq(x, axis, fmt="e4m3"):
    dtype, down = {"e4m3": (ml_dtypes.float8_e4m3fn, 7), "e5m2": (ml_dtypes.float8_e5m2, 14)}[fmt]
    v = np.moveaxis(np.asarray(x, np.float32).astype(ml_dtypes.bfloat16).astype(np.float64), axis, -1)
    blocks = v.reshape(v.shape[:-1] + (-1, 32))
    amax = np.abs(blocks).max(-1, keepdims=True)
    byte = np.maximum(np.where(amax > 0, np.frexp(amax)[1] - 1 + 127, 0) - down, 1)
    scale = np.exp2(byte - 127.0)
    codes = (blocks / scale).astype(np.float32).astype(dtype).astype(np.float64)
    return np.moveaxis((codes * scale).reshape(v.shape), -1, axis)


WIDE = False


def mx_kscale(k):
    if not WIDE:
        return np.ones(k)
    levels = np.array([10, -10, 5, -5, 0])
    if k % 512:
        return np.exp2(np.random.permutation(np.resize(levels, k // 32))).repeat(32)
    a = np.empty((k // 512, 16))
    for p in range(k // 512):
        a[p, :8] = np.random.permutation(np.resize(levels, 8))
        for g in range(8):
            far = levels[np.abs(levels - a[p, g]) >= 10]
            a[p, g + 8] = far[np.random.randint(len(far))]
    return np.exp2(a.ravel()).repeat(32)


BF16 = ml_dtypes.bfloat16


def bf(x):
    return np.asarray(x, np.float32).astype(BF16)


def f64(x):
    return np.asarray(x).astype(np.float64)


E2M1 = np.array([0.0, 0.5, 1.0, 1.5, 2.0, 3.0, 4.0, 6.0, -0.0, -0.5, -1.0, -1.5, -2.0, -3.0, -4.0, -6.0])


def pack_weight(w, fmt):
    k, n = w.shape
    w = f64(bf(w)).reshape(k // 32, 32, n)
    amax = np.abs(w).max(1)
    if fmt == "e4m3":
        byte = np.frexp(amax)[1] - 1 + 127 - 7
    else:
        mant, ex = np.frexp(amax / 6.0)
        byte = np.where(mant > 0.5, ex, ex - 1) + 127
    byte = np.clip(np.where(amax > 0, byte, 1), 1, 254)
    scaled = (w * np.exp2(127.0 - byte)[:, None, :]).reshape(k, n).astype(np.float32)
    by_word = np.ascontiguousarray(scaled.reshape(k // 512, 128, 4, n).transpose(0, 1, 3, 2))
    if fmt == "e4m3":
        words = by_word.astype(ml_dtypes.float8_e4m3fn).view(np.uint8)
    else:
        c = by_word.astype(ml_dtypes.float4_e2m1fn).view(np.uint8) & 0xF
        words = c[..., 0::2] | (c[..., 1::2] << 4)
    return np.ascontiguousarray(words), np.ascontiguousarray(byte.astype(np.uint8).reshape(k // 512, 16, n))


def unpack_weight(words, scales, fmt):
    g, p, n, _ = words.shape
    if fmt == "e4m3":
        vals = np.ascontiguousarray(words).view(ml_dtypes.float8_e4m3fn).astype(np.float64)
    else:
        nib = np.empty((g, p, n, 4), np.uint8)
        nib[..., 0::2] = words & 0xF
        nib[..., 1::2] = words >> 4
        vals = E2M1[nib]
    vals = vals * np.repeat(np.exp2(scales.astype(np.float64) - 127.0), 8, axis=1)[..., None]
    return vals.transpose(0, 1, 3, 2).reshape(g * 512, n)
def pack4(w):
    words, scales = pack_weight(w, "e2m1")
    return words.reshape(words.shape[0], 128, -1), scales


def unpack4(words, scales):
    return unpack_weight(words.reshape(words.shape[0], 128, -1, 2), scales, "e2m1")


M, N, K, D, R = 1024, 1024, 1024, 2048, 512


def setup_inputs():
    s, t, u = mx_kscale(K), mx_kscale(N), mx_kscale(M)
    a = np.random.standard_normal((M, K)) * s * u[:, None]
    b = np.random.standard_normal((N, K)) / np.sqrt(K) / s
    inv = np.exp(0.3 * np.random.standard_normal(N)) * t
    grad = np.random.standard_normal((M, D)) * u[:, None]
    v_words, v_scales = pack4(np.random.standard_normal((N, D)) / np.sqrt(N) / t[:, None])
    mix = np.random.standard_normal((R, M)) / np.sqrt(M) / u
    return {"a": bf(a), "b": bf(b), "inv": bf(inv), "grad": bf(grad),
            "v_words": v_words, "v_scales": v_scales, "mix": bf(mix)}


def reference(a, b, inv, grad, v_words, v_scales, mix):
    gram = mxq(f64(a), 1, "e4m3") @ mxq(f64(b), 1, "e4m3").T
    h = np.minimum(gram, 0.0) * f64(inv)
    fixed = f64(grad) - (mxq(h, 1, "e4m3") @ unpack4(v_words, v_scales))
    charge = mxq(f64(mix), 1, "e4m3") @ mxq(h, 0, "e4m3")
    return fixed, charge

@@ -1,0 +1,239 @@
+from contextlib import ExitStack
+
+import concourse.mybir as mybir
+from concourse.masks import make_identity
+
+M, N, K, D, R = 1024, 1024, 1024, 2048, 512
+FLOPS = 2 * M * N * K + 2 * M * N * D + 2 * R * M * N
+
+F32 = mybir.dt.float32
+BF16 = mybir.dt.bfloat16
+I32 = mybir.dt.int32
+U32 = mybir.dt.uint32
+U8 = mybir.dt.uint8
+FP8X4 = mybir.dt.float8_e4m3fn_x4
+FP4X4 = mybir.dt.float4_e2m1fn_x4
+ACT = mybir.ActivationFunctionType
+ALU = mybir.AluOpType
+P = 128
+
+ORDER = """
+Linv:D La001:D La012:D La023:D La034:D Lb002:D Lb024:D Lb102:D Lb124:D Lvs:D La104:D Lv:D Lg0:D Lm004:D Lg1:D
+Lg2:D Lg3:D Ninv:V Ta0:P Ta1:P Ea0:S Ta2:P Ea1:S Qa0:V Ta3:P Ea2:S Qa1:V Ea3:S Qa2:V Tb0:P Qa3:V Tb1:P Eb0:S
+Tb2:P Eb1:S Qb0:V Tb3:P Eb2:S Qb1:V G00:P Eb3:S Qb2:V G01:P R00:S Qb3:V Tb4:P R01:S Tb5:P Eb4:S G02:P Eb5:S
+Qb4:V G03:P R02:S Qb5:V Tb6:P R03:S Tb7:P Eb6:S I000:V G04:P Eb7:S G05:P Qb6:V X000:V R04:S G06:P Qb7:V I001:V
+R05:S G07:P R06:S Ta4:P X001:V R07:S Ta5:P Ea4:S Ta6:P I010:V Ea5:S Ta7:P Qa4:V Ea6:S H000:P X010:V Qa5:V
+H001:P Ea7:S Qa6:V W00:P I011:V J000:S W01:P J001:S Qa7:V W02:P F00:V W03:P F01:V G10:P F02:V G11:P F03:V
+R10:S G12:P X011:V Y00:V R11:S G13:P R12:S W10:P R13:S W11:P F10:V W12:P F11:V W13:P S002:D F12:V G14:P F13:V
+G15:P S024:D R14:S I100:V G16:P R15:S G17:P I101:V S102:D R16:S W20:P X100:V X101:V R17:S W21:P S124:D F20:V
+W22:P F21:V W23:P F22:V H010:P H011:P F23:V S202:D H100:P J010:S I110:V H101:P H110:P J011:S I111:V H111:P
+S224:D J100:S W30:P X110:V J101:S X111:V W31:P Y01:V J110:S W32:P F30:V J111:S W33:P F31:V W40:P F32:V W41:P
+F33:V S302:D W42:P F40:V W43:P F41:V S324:D W50:P F42:V W51:P F43:V S402:D W52:P F50:V W53:P F51:V W60:P
+S424:D F52:V W61:P F53:V W62:P S502:D F60:V W63:P F61:V Tm0:P S524:D F62:V Tm1:P F63:V Em0:S W70:P Y10:V
+S602:D Em1:S W71:P Qm0:V Y11:V W72:P S624:D F70:V W73:P F71:V Tm2:P F72:V Tm3:P F73:V Em2:S S702:D C00:P Qm1:V
+Em3:S Qm2:V C01:P S724:D K00:S Qm3:V C10:P K01:S C11:P K10:S C20:P K11:S C21:P Z002:D K20:S C30:P K21:S C31:P
+Z102:D K30:S K31:S Z202:D Z301:D Z312:D
+""".split()
+PERMUTED = "".split()
+OUT_BUFS = 5
+
+
+def tile_conflict_gradient_surgery_s8_kernel(tc, a, b, inv, grad, v_words, v_scales, mix, out_0, out_1):
+    nc = tc.nc
+    with ExitStack() as ctx:
+        keep = ctx.enter_context(tc.tile_pool(name="keep", bufs=1))
+        stage = ctx.enter_context(tc.tile_pool(name="stage", bufs=1))
+        psum = ctx.enter_context(tc.psum_pool(name="psum", bufs=1))
+        ctx.enter_context(tc.manual_schedule())
+
+        def kept(name, shape, dtype):
+            return keep.tile(shape, dtype, name=name, align_bytes=64)
+
+        raw = {
+            "a": [kept("a_raw%d" % g, [P, 4, K], BF16) for g in range(2)],
+            "b": [kept("b_raw%d" % g, [P, 4, K], BF16) for g in range(2)],
+            "m": [kept("mix_raw", [P, 4, M], BF16)],
+        }
+        src = {"a": a, "b": b, "m": mix}
+        grad_sb = [kept("grad%d" % n, [P, 2, D], BF16) for n in range(4)]
+        v_codes = kept("v_codes", [P, 2, 2 * D], U8)
+        v_plane = kept("v_plane", [P, 2, D], U8)
+        inv_sb = kept("inv_sb", [P, 2, 4], BF16)
+        neg_inv = kept("neg_inv", [P, 2, 4], F32)
+        ident = kept("ident", [P, P], F32)
+        warm = kept("warm", [P, 8], F32)
+        warm_out = kept("warm_out", [P, 8], F32)
+
+        def mx_tiles(name, count, width):
+            return [(kept("%s_codes%d" % (name, i), [P, width], U32), kept("%s_plane%d" % (name, i), [P, width], U8))
+                    for i in range(count)]
+
+        a_mx = mx_tiles("a", 4, 512)
+        b_mx = mx_tiles("b", 8, 256)
+        m_mx = mx_tiles("m", 4, 256)
+        hj_mx = mx_tiles("hj", 4, 512)
+        hi_mx = mx_tiles("hi", 4, 512)
+        h_plain = [kept("h_plain%d" % i, [P, 4, 512], BF16) for i in range(4)]
+        zero_mx = mx_tiles("z", 1 if "O:V" in ORDER else 0, 512)
+        live = {}
+        banks = []
+
+        def new_bank(key):
+            tag = "bank%d" % (len(banks) % 8)
+            banks.append(key)
+            live[key] = psum.tile([P, 512], F32, name=tag, tag=tag)
+            return live[key]
+
+        def quantize(pair, lo, width, values):
+            nc.vector.quantize_mx(out=pair[0][:, lo:lo + width].bitcast(FP8X4), scales=pair[1][:, lo:lo + width], in_=values)
+
+        def copy(eng, out, in_):
+            if eng == "V":
+                nc.vector.tensor_copy(out=out, in_=in_)
+            else:
+                nc.scalar.copy(out=out, in_=in_)
+
+        def mx_group(bank, passes):
+            for i, (lhs, lcols, rhs, rscale) in enumerate(passes):
+                nc.tensor.matmul_mx(out=bank, lhsT=lhs[0][:, lcols].bitcast(FP8X4), lhsT_scale=lhs[1][:, lcols],
+                                    rhs=rhs, rhs_scale=rscale, start=(i == 0), stop=(i == len(passes) - 1))
+
+        def step(name, eng):
+            kind = name[0]
+            if name == "Linv":
+                nc.scalar.dma_start(out=inv_sb[:], in_=inv.rearrange("(g p t) -> p g t", g=2, t=4))
+                nc.vector.memset(warm[:], 0.0)
+                nc.scalar.activation(out=warm_out[:], in_=warm[:], func=ACT.Relu)
+                make_identity(nc, ident[:])
+                nc.gpsimd.memset(v_plane[:].rearrange("p g n -> p (g n)").bitcast(I32), 0)
+            elif name == "Ninv":
+                nc.vector.tensor_scalar(out=neg_inv[:], in0=inv_sb[:], scalar1=-1.0, scalar2=None, op0=ALU.mult)
+            elif name == "Lvs":
+                for q in range(4):
+                    nc.sync.dma_start(out=v_plane[32 * q:32 * q + 4, :, :].bitcast(I32),
+                                      in_=v_scales[:, 4 * q:4 * q + 4, :].rearrange("g r n -> r g n").bitcast(I32))
+            elif name == "Lv":
+                nc.sync.dma_start(out=v_codes[:].bitcast(I32), in_=v_words.rearrange("g p n -> p g n").bitcast(I32))
+            elif name[:2] == "Lg":
+                n = int(name[2])
+                nc.sync.dma_start(out=grad_sb[n][:], in_=grad[256 * n:256 * (n + 1), :].rearrange("(c p) d -> p c d", c=2))
+            elif kind == "L":
+                x, g, lo, hi = name[1], int(name[2]), int(name[3]), int(name[4])
+                rows = src[x][512 * g:512 * (g + 1), :].rearrange("(m t) k -> m t k", t=4)
+                nc.sync.dma_start(out=raw[x][g][:, lo:hi, :], in_=rows[:, lo:hi, :])
+            elif kind == "O":
+                zeros = stage.tile([P, 2048], BF16, name="zeros", tag="wide", bufs=3, align_bytes=64)
+                nc.vector.memset(zeros[:], 0.0)
+                quantize(zero_mx[0], 0, 512, zeros[:])
+            elif kind == "D":
+                width = 128 * int(name[1])
+                bank = new_bank(name)
+                for i in range(int(name[2])):
+                    mx_group(bank[:, 0:width], [(zero_mx[0], slice(0, P), zero_mx[0][0][:, 0:width].bitcast(FP8X4), zero_mx[0][1][:, 0:width])])
+            elif kind == "P":
+                x, n = name[1], int(name[2])
+                words = raw[x][n // 4][:, n % 4, :].bitcast(F32)
+                split = stage.tile([P, 512], F32, name="split", tag="split", bufs=3, align_bytes=64)
+                copy(eng, split[:].rearrange("r (g u p) -> r g u p", g=2, u=2), words.rearrange("r (g p u) -> r g u p", g=2, u=2))
+                live[name] = split
+            elif kind == "T":
+                x, n = name[1], int(name[2])
+                bank = new_bank(name)
+                for g in range(2):
+                    for u in range(2):
+                        if name[1:] in PERMUTED:
+                            words = live["P" + name[1:]][:, 256 * g + P * u:256 * g + P * (u + 1)]
+                        else:
+                            words = raw[x][n // 4][:, n % 4, :].bitcast(F32)[:, 256 * g + u:256 * (g + 1):2]
+                        nc.tensor.transpose(bank[:, 256 * g + P * u:256 * g + P * (u + 1)], words, ident[:])
+            elif kind == "E":
+                grouped = stage.tile([P, 1024], BF16, name="grouped", tag="grouped", bufs=6, align_bytes=64)
+                copy(eng, grouped[:].bitcast(F32).rearrange("p (g r u) -> p g r u", g=2, u=2),
+                     live["T" + name[1:]][:].rearrange("p (g u r) -> p g r u", g=2, u=2))
+                live[name] = grouped
+            elif kind == "Q":
+                x, n = name[1], int(name[2])
+                grouped = live["E" + name[1:]]
+                if x == "a":
+                    for g in range(2):
+                        quantize(a_mx[2 * (n // 4) + g], P * (n % 4), P, grouped[:, 512 * g:512 * (g + 1)])
+                else:
+                    quantize((b_mx if x == "b" else m_mx)[n], 0, 256, grouped[:])
+            elif kind == "G":
+                g, n = int(name[1]), int(name[2])
+                mx_group(new_bank(name)[:], [(b_mx[n], slice(P * c, P * (c + 1)), a_mx[2 * g + c][0][:].bitcast(FP8X4), a_mx[2 * g + c][1][:])
+                                             for c in range(2)])
+            elif kind == "R":
+                g, n = int(name[1]), int(name[2])
+                out = h_plain[2 * g + n // 4][:, n % 4, :].rearrange("p (u m e) -> p u m e", u=2, e=2)
+                in_ = live["G" + name[1:]][:].rearrange("p (u e m) -> p u m e", u=2, e=2)
+                factor = neg_inv[:, n // 4, n % 4:n % 4 + 1]
+                if eng == "S":
+                    nc.scalar.activation(out=out, in_=in_, func=ACT.Relu, scale=factor)
+                else:
+                    nc.vector.tensor_scalar(out=out, in0=in_, scalar1=factor, scalar2=0.0, op0=ALU.mult, op1=ALU.max)
+            elif kind == "I":
+                g, j, half = int(name[1]), int(name[2]), int(name[3])
+                grouped = stage.tile([P, 1024], BF16, name="grouped", tag="grouped", bufs=6, align_bytes=64)
+                plain = h_plain[2 * g + j][:].rearrange("p t (u m e) -> p m u e t", u=2, e=2)
+                copy(eng, grouped[:].rearrange("p (m u e t) -> p m u e t", u=2, e=2, t=4), plain[:, 64 * half:64 * (half + 1)])
+                live[name] = grouped
+            elif kind == "X":
+                g, j, half = int(name[1]), int(name[2]), int(name[3])
+                quantize(hj_mx[2 * g + j], 256 * half, 256, live["I" + name[1:]][:])
+            elif kind == "H":
+                g, j, half = int(name[1]), int(name[2]), int(name[3])
+                bank = new_bank(name)
+                for tt in range(2):
+                    words = h_plain[2 * g + j][:, 2 * half + tt, :].bitcast(F32)
+                    for u in range(2):
+                        nc.tensor.transpose(bank[:, 256 * tt + P * u:256 * tt + P * (u + 1)], words[:, P * u:P * (u + 1)], ident[:])
+            elif kind == "J":
+                g, j, half = int(name[1]), int(name[2]), int(name[3])
+                key = "wide%d%d" % (g, j)
+                if key not in live:
+                    live[key] = stage.tile([P, 2048], BF16, name="wide", tag="wide", bufs=3, align_bytes=64)
+                copy(eng, live[key][:, 1024 * half:1024 * (half + 1)].bitcast(F32).rearrange("p (g r u) -> p g r u", g=2, u=2),
+                     live["H" + name[1:]][:].rearrange("p (g u r) -> p g r u", g=2, u=2))
+            elif kind == "Y":
+                g, j = int(name[1]), int(name[2])
+                quantize(hi_mx[2 * g + j], 0, 512, live["wide%d%d" % (g, j)][:])
+            elif kind == "W":
+                n, q = int(name[1]), int(name[2])
+                cols = slice(P * (n % 4), P * (n % 4 + 1))
+                mx_group(new_bank(name)[:], [(hj_mx[2 * (n // 4) + j], cols, v_codes[:, j, 1024 * q:1024 * (q + 1)].bitcast(FP4X4),
+                                              v_plane[:, j, 512 * q:512 * (q + 1)]) for j in range(2)])
+            elif kind == "F":
+                n, q = int(name[1]), int(name[2])
+                key = "fixed%d" % n
+                if key not in live:
+                    live[key] = stage.tile([P, D], F32, name="fixed", tag="fixed", bufs=OUT_BUFS, align_bytes=64)
+                cols = slice(512 * q, 512 * (q + 1))
+                nc.vector.tensor_tensor(out=live[key][:, cols], in0=live["W" + name[1:]][:], in1=grad_sb[n // 2][:, n % 2, cols], op=ALU.add)
+            elif kind == "S":
+                n, lo, hi = int(name[1]), int(name[2]), int(name[3])
+                cols = slice(512 * lo, 512 * hi)
+                nc.sync.dma_start(out=out_0[P * n:P * (n + 1), cols], in_=live["fixed%d" % n][:, cols])
+            elif kind == "C":
+                r, j = int(name[1]), int(name[2])
+                mx_group(new_bank(name)[:], [(m_mx[r], slice(P * g, P * (g + 1)), hi_mx[2 * g + j][0][:].bitcast(FP8X4), hi_mx[2 * g + j][1][:])
+                                             for g in range(2)])
+            elif kind == "K":
+                r, j = int(name[1]), int(name[2])
+                key = "charge%d" % r
+                if key not in live:
+                    live[key] = keep.tile([P, N], F32, name=key, align_bytes=64)
+                out = live[key][:, 512 * j:512 * (j + 1)].rearrange("p (m t) -> p m t", t=4)
+                in_ = live["C" + name[1:]][:].rearrange("p (t m) -> p m t", t=4)
+                if eng == "S":
+                    nc.scalar.activation(out=out, in_=in_, func=ACT.Copy, scale=-1.0)
+                else:
+                    nc.vector.tensor_scalar(out=out, in0=in_, scalar1=-1.0, scalar2=None, op0=ALU.mult)
+            elif kind == "Z":
+                r, lo, hi = int(name[1]), int(name[2]), int(name[3])
+                rows = out_1.rearrange("(m t) n -> m t n", t=4)
+                nc.sync.dma_start(out=rows[:, r, 512 * lo:512 * hi], in_=live["charge%d" % r][:, 512 * lo:512 * hi])
+
+        for item in ORDER:
+            parts = item.split(":")
+            step(parts[0], parts[1])

@@ -18,24 +18,25 @@ ALU = mybir.AluOpType
 P = 128
 
 ORDER = """
-Linv:D La001:D La012:D La023:D La034:D Lb002:D Lb024:D Lb102:D Lb124:D Lvs:D La104:D Lv:D Lg0:D Lm004:D Lg1:D
-Lg2:D Lg3:D Ninv:V Ta0:P Ta1:P Ea0:S Ta2:P Ea1:S Qa0:V Ta3:P Ea2:S Qa1:V Ea3:S Qa2:V Tb0:P Qa3:V Tb1:P Eb0:S
-Tb2:P Eb1:S Qb0:V Tb3:P Eb2:S Qb1:V G00:P Eb3:S Qb2:V G01:P R00:S Qb3:V Tb4:P R01:S Tb5:P Eb4:S G02:P Eb5:S
-Qb4:V G03:P R02:S Qb5:V Tb6:P R03:S Tb7:P Eb6:S I000:V G04:P Eb7:S G05:P Qb6:V X000:V R04:S G06:P Qb7:V I001:V
-R05:S G07:P R06:S Ta4:P X001:V R07:S Ta5:P Ea4:S Ta6:P I010:V Ea5:S Ta7:P Qa4:V Ea6:S H000:P X010:V Qa5:V
-H001:P Ea7:S Qa6:V W00:P I011:V J000:S W01:P J001:S Qa7:V W02:P F00:V W03:P F01:V G10:P F02:V G11:P F03:V
-R10:S G12:P X011:V Y00:V R11:S G13:P R12:S W10:P R13:S W11:P F10:V W12:P F11:V W13:P S002:D F12:V G14:P F13:V
-G15:P S024:D R14:S I100:V G16:P R15:S G17:P I101:V S102:D R16:S W20:P X100:V X101:V R17:S W21:P S124:D F20:V
-W22:P F21:V W23:P F22:V H010:P H011:P F23:V S202:D H100:P J010:S I110:V H101:P H110:P J011:S I111:V H111:P
-S224:D J100:S W30:P X110:V J101:S X111:V W31:P Y01:V J110:S W32:P F30:V J111:S W33:P F31:V W40:P F32:V W41:P
-F33:V S302:D W42:P F40:V W43:P F41:V S324:D W50:P F42:V W51:P F43:V S402:D W52:P F50:V W53:P F51:V W60:P
-S424:D F52:V W61:P F53:V W62:P S502:D F60:V W63:P F61:V Tm0:P S524:D F62:V Tm1:P F63:V Em0:S W70:P Y10:V
-S602:D Em1:S W71:P Qm0:V Y11:V W72:P S624:D F70:V W73:P F71:V Tm2:P F72:V Tm3:P F73:V Em2:S S702:D C00:P Qm1:V
-Em3:S Qm2:V C01:P S724:D K00:S Qm3:V C10:P K01:S C11:P K10:S C20:P K11:S C21:P Z002:D K20:S C30:P K21:S C31:P
-Z102:D K30:S K31:S Z202:D Z301:D Z312:D
+Linv:D La001:D La012:D La023:D La034:D Lb001:D Lb012:D Lb024:D Lb102:D Lb124:D La104:D Lvs:D Lv:D Lg0:D Lg1:D
+Lg2:D Lm004:D Lg3:D O:V D28c:P Ninv:V Pa0:V Pa1:V Ta0:P Ta1:P Pa2:V Ea0:S D24a:P Pa3:V Ea1:S Qa0:V Ta2:P Pb0:V
+Ta3:P Qa1:V Tb0:P Ea2:S Pb1:V D24b:P Ea3:S Qa2:V Tb1:P Eb0:S Qa3:V Pb2:V Pb3:V Eb1:S Tb2:P Qb0:V Tb3:P Qb1:V
+G00:P Eb2:S Pb4:V Pb5:V G01:P Eb3:V R00:S Pb6:V Tb4:P Pb7:V Tb5:P R01:S Qb2:V Tb6:P Qb3:V Eb4:S Tb7:P Eb5:V
+G02:P Eb6:S Qb4:V G03:P Eb7:V R02:S G04:P Qb5:V Qb6:V R03:S G05:P Pa4:V Qb7:V R04:S G06:P Pa5:V Pa6:V R05:S
+G07:P Pa7:V I000:V R06:S Ta4:P Ta5:P I001:V R07:S Ta6:P Ta7:P Ea4:S X000:V H000:P I010:V Ea5:S H001:P H010:P
+Qa4:V Ea6:S H011:P X010:V Ea7:S Qa5:V W00:P Qa6:V J000:S Qa7:V W01:P J001:S F00:V W02:P J010:S F01:V W03:P
+J011:S F02:V G10:P F03:V G11:P R10:S X001:V G12:P I011:V R11:S G13:P Y00:V R12:S G14:P X011:V R13:S G15:P
+Y01:V G16:P R14:S I100:V G17:P R15:S W10:P R16:S S002:D W11:P R17:S F10:V W12:P S024:D I110:S F11:V W13:P
+F12:V W20:P F13:V I101:S W21:P S102:D X100:V W22:P F20:V W23:P I111:S S124:D F21:V H100:P F22:V H101:P F23:V
+H110:P J100:S S202:D H111:P X110:V J101:S W30:P X101:V X111:V J110:S W31:P S224:D J111:S F30:V W32:P Pm0:S
+F31:V W33:P Pm1:S F32:V W40:P Pm2:S F33:V W41:P S302:D Pm3:S Y10:V W42:P Y11:V W43:P S324:D F40:V Tm0:P Tm1:P
+F41:V Tm2:P Em0:S F42:V Tm3:P Em1:S W50:P F43:V S402:D Em2:S W51:P Em3:S F50:V W52:P S424:D F51:V W53:P F52:V
+W60:P F53:V W61:P S502:D Qm0:V W62:P Qm1:V F60:V W63:P S524:D F61:V C00:P F62:V C01:P K00:S F63:V C10:P S602:D
+K01:S Qm2:V C11:P Qm3:V K10:S W70:P S624:D K11:S W71:P F70:V W72:P Z002:D F71:V W73:P F72:V C20:P Z102:D F73:V
+C21:P K20:S C30:P S702:D K21:S C31:P K30:S K31:S S724:D Z202:D Z301:D Z312:D
 """.split()
-PERMUTED = "".split()
-OUT_BUFS = 5
+PERMUTED = "a0 a1 a2 a3 a4 a5 a6 a7 b0 b1 b2 b3 b4 b5 b6 b7 m0 m1 m2 m3".split()
+OUT_BUFS = 4
 
 
 def tile_conflict_gradient_surgery_s8_kernel(tc, a, b, inv, grad, v_words, v_scales, mix, out_0, out_1):
@@ -74,7 +75,7 @@ def tile_conflict_gradient_surgery_s8_kernel(tc, a, b, inv, grad, v_words, v_sca
         hj_mx = mx_tiles("hj", 4, 512)
         hi_mx = mx_tiles("hi", 4, 512)
         h_plain = [kept("h_plain%d" % i, [P, 4, 512], BF16) for i in range(4)]
-        zero_mx = mx_tiles("z", 1 if "O:V" in ORDER else 0, 512)
+        zero_mx = mx_tiles("z", 1 if "O:V" in ORDER else 0, 256)
         live = {}
         banks = []
 
@@ -122,9 +123,9 @@ def tile_conflict_gradient_surgery_s8_kernel(tc, a, b, inv, grad, v_words, v_sca
                 rows = src[x][512 * g:512 * (g + 1), :].rearrange("(m t) k -> m t k", t=4)
                 nc.sync.dma_start(out=raw[x][g][:, lo:hi, :], in_=rows[:, lo:hi, :])
             elif kind == "O":
-                zeros = stage.tile([P, 2048], BF16, name="zeros", tag="wide", bufs=3, align_bytes=64)
-                nc.vector.memset(zeros[:], 0.0)
-                quantize(zero_mx[0], 0, 512, zeros[:])
+                zeros = stage.tile([P, 1024], BF16, name="zeros", tag="grouped", bufs=7, align_bytes=64)
+                nc.vector.memset(zeros[:].bitcast(I32), 0)
+                quantize(zero_mx[0], 0, 256, zeros[:])
             elif kind == "D":
                 width = 128 * int(name[1])
                 bank = new_bank(name)
@@ -133,7 +134,7 @@ def tile_conflict_gradient_surgery_s8_kernel(tc, a, b, inv, grad, v_words, v_sca
             elif kind == "P":
                 x, n = name[1], int(name[2])
                 words = raw[x][n // 4][:, n % 4, :].bitcast(F32)
-                split = stage.tile([P, 512], F32, name="split", tag="split", bufs=3, align_bytes=64)
+                split = stage.tile([P, 512], F32, name="split", tag="split", bufs=5, align_bytes=64)
                 copy(eng, split[:].rearrange("r (g u p) -> r g u p", g=2, u=2), words.rearrange("r (g p u) -> r g u p", g=2, u=2))
                 live[name] = split
             elif kind == "T":
@@ -147,7 +148,7 @@ def tile_conflict_gradient_surgery_s8_kernel(tc, a, b, inv, grad, v_words, v_sca
                             words = raw[x][n // 4][:, n % 4, :].bitcast(F32)[:, 256 * g + u:256 * (g + 1):2]
                         nc.tensor.transpose(bank[:, 256 * g + P * u:256 * g + P * (u + 1)], words, ident[:])
             elif kind == "E":
-                grouped = stage.tile([P, 1024], BF16, name="grouped", tag="grouped", bufs=6, align_bytes=64)
+                grouped = stage.tile([P, 1024], BF16, name="grouped", tag="grouped", bufs=7, align_bytes=64)
                 copy(eng, grouped[:].bitcast(F32).rearrange("p (g r u) -> p g r u", g=2, u=2),
                      live["T" + name[1:]][:].rearrange("p (g u r) -> p g r u", g=2, u=2))
                 live[name] = grouped
@@ -174,9 +175,9 @@ def tile_conflict_gradient_surgery_s8_kernel(tc, a, b, inv, grad, v_words, v_sca
                     nc.vector.tensor_scalar(out=out, in0=in_, scalar1=factor, scalar2=0.0, op0=ALU.mult, op1=ALU.max)
             elif kind == "I":
                 g, j, half = int(name[1]), int(name[2]), int(name[3])
-                grouped = stage.tile([P, 1024], BF16, name="grouped", tag="grouped", bufs=6, align_bytes=64)
-                plain = h_plain[2 * g + j][:].rearrange("p t (u m e) -> p m u e t", u=2, e=2)
-                copy(eng, grouped[:].rearrange("p (m u e t) -> p m u e t", u=2, e=2, t=4), plain[:, 64 * half:64 * (half + 1)])
+                grouped = stage.tile([P, 1024], BF16, name="grouped", tag="grouped", bufs=7, align_bytes=64)
+                plain = h_plain[2 * g + j][:].rearrange("p t (u m e) -> p u m e t", u=2, e=2)
+                copy(eng, grouped[:].rearrange("p (m u e t) -> p u m e t", u=2, e=2, t=4), plain[:, :, 64 * half:64 * (half + 1)])
                 live[name] = grouped
             elif kind == "X":
                 g, j, half = int(name[1]), int(name[2]), int(name[3])

@@ -18,22 +18,22 @@ ALU = mybir.AluOpType
 P = 128
 
 ORDER = """
-Linv:D La001:D La012:D La023:D La034:D Lb001:D Lb012:D Lb024:D Lb102:D Lb124:D La104:D Lvs:D Lv:D Lg0:D Lg1:D
-Lg2:D Lm004:D Lg3:D O:V D28c:P Ninv:V Pa0:V Pa1:V Ta0:P Ta1:P Pa2:V Ea0:S D24a:P Pa3:V Ea1:S Qa0:V Ta2:P Pb0:V
-Ta3:P Qa1:V Tb0:P Ea2:S Pb1:V D24b:P Ea3:S Qa2:V Tb1:P Eb0:S Qa3:V Pb2:V Pb3:V Eb1:S Tb2:P Qb0:V Tb3:P Qb1:V
-G00:P Eb2:S Pb4:V Pb5:V G01:P Eb3:V R00:S Pb6:V Tb4:P Pb7:V Tb5:P R01:S Qb2:V Tb6:P Qb3:V Eb4:S Tb7:P Eb5:V
-G02:P Eb6:S Qb4:V G03:P Eb7:V R02:S G04:P Qb5:V Qb6:V R03:S G05:P Pa4:V Qb7:V R04:S G06:P Pa5:V Pa6:V R05:S
-G07:P Pa7:V I000:V R06:S Ta4:P Ta5:P I001:V R07:S Ta6:P Ta7:P Ea4:S X000:V H000:P I010:V Ea5:S H001:P H010:P
-Qa4:V Ea6:S H011:P X010:V Ea7:S Qa5:V W00:P Qa6:V J000:S Qa7:V W01:P J001:S F00:V W02:P J010:S F01:V W03:P
-J011:S F02:V G10:P F03:V G11:P R10:S X001:V G12:P I011:V R11:S G13:P Y00:V R12:S G14:P X011:V R13:S G15:P
-Y01:V G16:P R14:S I100:V G17:P R15:S W10:P R16:S S002:D W11:P R17:S F10:V W12:P S024:D I110:S F11:V W13:P
-F12:V W20:P F13:V I101:S W21:P S102:D X100:V W22:P F20:V W23:P I111:S S124:D F21:V H100:P F22:V H101:P F23:V
-H110:P J100:S S202:D H111:P X110:V J101:S W30:P X101:V X111:V J110:S W31:P S224:D J111:S F30:V W32:P Pm0:S
-F31:V W33:P Pm1:S F32:V W40:P Pm2:S F33:V W41:P S302:D Pm3:S Y10:V W42:P Y11:V W43:P S324:D F40:V Tm0:P Tm1:P
-F41:V Tm2:P Em0:S F42:V Tm3:P Em1:S W50:P F43:V S402:D Em2:S W51:P Em3:S F50:V W52:P S424:D F51:V W53:P F52:V
-W60:P F53:V W61:P S502:D Qm0:V W62:P Qm1:V F60:V W63:P S524:D F61:V C00:P F62:V C01:P K00:S F63:V C10:P S602:D
-K01:S Qm2:V C11:P Qm3:V K10:S W70:P S624:D K11:S W71:P F70:V W72:P Z002:D F71:V W73:P F72:V C20:P Z102:D F73:V
-C21:P K20:S C30:P S702:D K21:S C31:P K30:S K31:S S724:D Z202:D Z301:D Z312:D
+Linv:D O:V M:V La001:D La012:D La023:D La034:D Lb001:D Lb012:D Lb023:D Lb034:D Lb102:D Lb124:D La104:D Lvs:D
+Lv:D Lg0:D Lg1:D Lm004:D Lg2:D Lg3:D D27c:P Ninv:V Pa0:V Pa1:V Ta0:P Ta1:P Pa2:V Ea0:S D24a:P Pa3:V Ea1:S
+Ta2:P Qa0:V Ta3:P Pb0:V Qa1:V Ea2:S Tb0:P Pb1:V D24b:P Ea3:S Qa2:V Pb2:V Eb0:S Tb1:P Qa3:V Tb2:P Pb3:V Eb1:S
+Qb0:V Tb3:P Eb2:S G00:P Qb1:V Pb4:V G01:P Pb5:V Eb3:V R00:S Tb4:P Tb5:P Pb6:V R01:S Pb7:V Tb6:P Eb4:S Qb2:V
+Tb7:P Qb3:V G02:P Eb6:S Eb5:V G03:P Qb4:V Eb7:V R02:S G04:P Qb5:V R03:S Qb6:V G05:P R04:S Qb7:V Pa4:V G06:P
+Pa5:V R05:S G07:P Pa6:V Pa7:V R06:S Ta4:P I000:V Ta5:P R07:S Ta6:P I001:V Ta7:P Ea4:S H000:P X000:V Ea5:S
+H001:P I010:V H010:P Ea6:S H011:P Qa4:V Ea7:S X010:V Qa5:V W00:P J000:S Qa6:V W01:P Qa7:V J001:S F00:V W02:P
+J010:S F01:V W03:P J011:S F02:V G10:P F03:V G11:P R10:S X001:V G12:P I011:V R11:S G13:P Y00:V R12:S G14:P
+X011:V G15:P R13:S Y01:V G16:P R14:S S002:D I100:V G17:P R15:S I101:V W10:P R16:S S024:D W11:P X100:V R17:S
+X101:V W12:P F10:V Pm0:S W13:P F11:V Pm1:S H100:P F12:V Pm2:S H101:P H110:P F13:V J100:S S102:D H111:P J101:S
+W20:P Pm3:S W21:P S124:D F20:V J110:S W22:P F21:V J111:S W23:P F22:V I110:S Tm0:P Tm1:P F23:V S202:D Tm2:P
+Y10:V Tm3:P Em0:S W30:P X110:V Em1:S S224:D Y11:V W31:P Em2:S F30:V W32:P Em3:S W33:P F31:V I111:S W40:P F32:V
+W41:P F33:V S302:D W42:P Qm0:V F40:V W43:P S324:D F41:V C00:P F42:V C01:P K00:S F43:V W50:P S402:D K01:S Qm1:V
+W51:P X111:V W52:P F50:V S424:D W53:P F51:V C10:P F52:V Z002:D C11:P F53:V K10:S W60:P Qm2:V S502:D K11:S
+W61:P F60:V W62:P S524:D F61:V W63:P F62:V C20:P Z102:D F63:V C21:P K20:S Qm3:V W70:P S602:D K21:S W71:P F70:V
+W72:P S624:D F71:V W73:P F72:V C30:P Z202:D F73:V C31:P K30:S S702:D K31:V S723:D S734:D Z301:D Z312:D
 """.split()
 PERMUTED = "a0 a1 a2 a3 a4 a5 a6 a7 b0 b1 b2 b3 b4 b5 b6 b7 m0 m1 m2 m3".split()
 OUT_BUFS = 4
@@ -106,7 +106,6 @@ def tile_conflict_gradient_surgery_s8_kernel(tc, a, b, inv, grad, v_words, v_sca
                 nc.vector.memset(warm[:], 0.0)
                 nc.scalar.activation(out=warm_out[:], in_=warm[:], func=ACT.Relu)
                 make_identity(nc, ident[:])
-                nc.gpsimd.memset(v_plane[:].rearrange("p g n -> p (g n)").bitcast(I32), 0)
             elif name == "Ninv":
                 nc.vector.tensor_scalar(out=neg_inv[:], in0=inv_sb[:], scalar1=-1.0, scalar2=None, op0=ALU.mult)
             elif name == "Lvs":
@@ -126,6 +125,8 @@ def tile_conflict_gradient_surgery_s8_kernel(tc, a, b, inv, grad, v_words, v_sca
                 zeros = stage.tile([P, 1024], BF16, name="zeros", tag="grouped", bufs=7, align_bytes=64)
                 nc.vector.memset(zeros[:].bitcast(I32), 0)
                 quantize(zero_mx[0], 0, 256, zeros[:])
+            elif kind == "M":
+                nc.vector.memset(v_plane[:].rearrange("p g n -> p (g n)").bitcast(I32), 0)
             elif kind == "D":
                 width = 128 * int(name[1])
                 bank = new_bank(name)
@@ -160,6 +161,12 @@ def tile_conflict_gradient_surgery_s8_kernel(tc, a, b, inv, grad, v_words, v_sca
                         quantize(a_mx[2 * (n // 4) + g], P * (n % 4), P, grouped[:, 512 * g:512 * (g + 1)])
                 else:
                     quantize((b_mx if x == "b" else m_mx)[n], 0, 256, grouped[:])
+            elif kind == "g":
+                n, half = int(name[2]), int(name[3])
+                bank = new_bank("G" + name[1:3]) if half == 0 else live["G" + name[1:3]]
+                cols = slice(256 * half, 256 * (half + 1))
+                mx_group(bank[:, cols], [(b_mx[n], slice(P * c, P * (c + 1)), a_mx[c][0][:, cols].bitcast(FP8X4), a_mx[c][1][:, cols])
+                                         for c in range(2)])
             elif kind == "G":
                 g, n = int(name[1]), int(name[2])
                 mx_group(new_bank(name)[:], [(b_mx[n], slice(P * c, P * (c + 1)), a_mx[2 * g + c][0][:].bitcast(FP8X4), a_mx[2 * g + c][1][:])

@@ -15,28 +15,20 @@ FP8X4 = mybir.dt.float8_e4m3fn_x4
 FP4X4 = mybir.dt.float4_e2m1fn_x4
 ACT = mybir.ActivationFunctionType
 ALU = mybir.AluOpType
-P = 128
 
-ORDER = """
-Linv:D O:V M:V La001:D La012:D La023:D La034:D Lb001:D Lb012:D Lb023:D Lb034:D Lb102:D Lb124:D La104:D Lvs:D
-Lv:D Lg0:D Lg1:D Lm004:D Lg2:D Lg3:D D27c:P Ninv:V Pa0:V Pa1:V Ta0:P Ta1:P Pa2:V Ea0:S D24a:P Pa3:V Ea1:S
-Ta2:P Qa0:V Ta3:P Pb0:V Qa1:V Ea2:S Tb0:P Pb1:V D24b:P Ea3:S Qa2:V Pb2:V Eb0:S Tb1:P Qa3:V Tb2:P Pb3:V Eb1:S
-Qb0:V Tb3:P Eb2:S G00:P Qb1:V Pb4:V G01:P Pb5:V Eb3:V R00:S Tb4:P Tb5:P Pb6:V R01:S Pb7:V Tb6:P Eb4:S Qb2:V
-Tb7:P Qb3:V G02:P Eb6:S Eb5:V G03:P Qb4:V Eb7:V R02:S G04:P Qb5:V R03:S Qb6:V G05:P R04:S Qb7:V Pa4:V G06:P
-Pa5:V R05:S G07:P Pa6:V Pa7:V R06:S Ta4:P I000:V Ta5:P R07:S Ta6:P I001:V Ta7:P Ea4:S H000:P X000:V Ea5:S
-H001:P I010:V H010:P Ea6:S H011:P Qa4:V Ea7:S X010:V Qa5:V W00:P J000:S Qa6:V W01:P Qa7:V J001:S F00:V W02:P
-J010:S F01:V W03:P J011:S F02:V G10:P F03:V G11:P R10:S X001:V G12:P I011:V R11:S G13:P Y00:V R12:S G14:P
-X011:V G15:P R13:S Y01:V G16:P R14:S S002:D I100:V G17:P R15:S I101:V W10:P R16:S S024:D W11:P X100:V R17:S
-X101:V W12:P F10:V Pm0:S W13:P F11:V Pm1:S H100:P F12:V Pm2:S H101:P H110:P F13:V J100:S S102:D H111:P J101:S
-W20:P Pm3:S W21:P S124:D F20:V J110:S W22:P F21:V J111:S W23:P F22:V I110:S Tm0:P Tm1:P F23:V S202:D Tm2:P
-Y10:V Tm3:P Em0:S W30:P X110:V Em1:S S224:D Y11:V W31:P Em2:S F30:V W32:P Em3:S W33:P F31:V I111:S W40:P F32:V
-W41:P F33:V S302:D W42:P Qm0:V F40:V W43:P S324:D F41:V C00:P F42:V C01:P K00:S F43:V W50:P S402:D K01:S Qm1:V
-W51:P X111:V W52:P F50:V S424:D W53:P F51:V C10:P F52:V Z002:D C11:P F53:V K10:S W60:P Qm2:V S502:D K11:S
-W61:P F60:V W62:P S524:D F61:V W63:P F62:V C20:P Z102:D F63:V C21:P K20:S Qm3:V W70:P S602:D K21:S W71:P F70:V
-W72:P S624:D F71:V W73:P F72:V C30:P Z202:D F73:V C31:P K30:S S702:D K31:V S723:D S734:D Z301:D Z312:D
-""".split()
-PERMUTED = "a0 a1 a2 a3 a4 a5 a6 a7 b0 b1 b2 b3 b4 b5 b6 b7 m0 m1 m2 m3".split()
-OUT_BUFS = 4
+P = 128
+PACK = 4
+GROUP = P * PACK
+PASSES = 2
+BANK = 512
+BANKS = 8
+HALF = 256
+ALIGN = 64
+
+SORTED_BUFS = 5
+GROUPED_BUFS = 7
+WIDE_BUFS = 3
+FIXED_BUFS = 4
 
 
 def tile_conflict_gradient_surgery_s8_kernel(tc, a, b, inv, grad, v_words, v_scales, mix, out_0, out_1):
@@ -48,200 +40,294 @@ def tile_conflict_gradient_surgery_s8_kernel(tc, a, b, inv, grad, v_words, v_sca
         ctx.enter_context(tc.manual_schedule())
 
         def kept(name, shape, dtype):
-            return keep.tile(shape, dtype, name=name, align_bytes=64)
-
-        raw = {
-            "a": [kept("a_raw%d" % g, [P, 4, K], BF16) for g in range(2)],
-            "b": [kept("b_raw%d" % g, [P, 4, K], BF16) for g in range(2)],
-            "m": [kept("mix_raw", [P, 4, M], BF16)],
-        }
-        src = {"a": a, "b": b, "m": mix}
-        grad_sb = [kept("grad%d" % n, [P, 2, D], BF16) for n in range(4)]
-        v_codes = kept("v_codes", [P, 2, 2 * D], U8)
-        v_plane = kept("v_plane", [P, 2, D], U8)
-        inv_sb = kept("inv_sb", [P, 2, 4], BF16)
-        neg_inv = kept("neg_inv", [P, 2, 4], F32)
-        ident = kept("ident", [P, P], F32)
-        warm = kept("warm", [P, 8], F32)
-        warm_out = kept("warm_out", [P, 8], F32)
+            return keep.tile(shape, dtype, name=name, align_bytes=ALIGN)
 
         def mx_tiles(name, count, width):
             return [(kept("%s_codes%d" % (name, i), [P, width], U32), kept("%s_plane%d" % (name, i), [P, width], U8))
                     for i in range(count)]
 
-        a_mx = mx_tiles("a", 4, 512)
-        b_mx = mx_tiles("b", 8, 256)
-        m_mx = mx_tiles("m", 4, 256)
-        hj_mx = mx_tiles("hj", 4, 512)
-        hi_mx = mx_tiles("hi", 4, 512)
-        h_plain = [kept("h_plain%d" % i, [P, 4, 512], BF16) for i in range(4)]
-        zero_mx = mx_tiles("z", 1 if "O:V" in ORDER else 0, 256)
+        source = {"a": a, "b": b, "mix": mix}
+        raw = {x: [kept("%s_raw%d" % (x, g), [P, PACK, K], BF16) for g in range(source[x].shape[0] // GROUP)]
+               for x in ("a", "b", "mix")}
+        grad_sb = [kept("grad%d" % i, [P, 2, D], BF16) for i in range(M // (2 * P))]
+        v_codes = kept("v_codes", [P, PASSES, 2 * D], U8)
+        v_plane = kept("v_plane", [P, PASSES, D], U8)
+        inv_sb = kept("inv_sb", [P, PASSES, PACK], BF16)
+        neg_inv = kept("neg_inv", [P, PASSES, PACK], F32)
+        ident = kept("ident", [P, P], F32)
+        table_out = kept("table_out", [P, 8], F32)
+
+        a_mx = mx_tiles("a", 2 * PASSES, BANK)
+        b_mx = mx_tiles("b", N // P, PASSES * P)
+        mix_mx = mx_tiles("mix", R // P, PASSES * P)
+        h_by_anchor = mx_tiles("hj", 2 * PASSES, BANK)
+        h_by_task = mx_tiles("hi", 2 * PASSES, BANK)
+        h_plain = [kept("h_plain%d" % i, [P, PACK, BANK], BF16) for i in range(2 * PASSES)]
+        zero_mx = mx_tiles("zero", 1, HALF)[0]
+        charge_sb = [kept("charge%d" % r, [P, N], F32) for r in range(R // P)]
+
         live = {}
-        banks = []
+        opened = []
 
         def new_bank(key):
-            tag = "bank%d" % (len(banks) % 8)
-            banks.append(key)
-            live[key] = psum.tile([P, 512], F32, name=tag, tag=tag)
+            tag = "bank%d" % (len(opened) % BANKS)
+            opened.append(key)
+            live[key] = psum.tile([P, BANK], F32, name=tag, tag=tag)
             return live[key]
 
-        def quantize(pair, lo, width, values):
-            nc.vector.quantize_mx(out=pair[0][:, lo:lo + width].bitcast(FP8X4), scales=pair[1][:, lo:lo + width], in_=values)
+        def new_grouped(key):
+            live[key] = stage.tile([P, PACK * HALF], BF16, name="grouped", tag="grouped", bufs=GROUPED_BUFS, align_bytes=ALIGN)
+            return live[key]
 
-        def copy(eng, out, in_):
-            if eng == "V":
-                nc.vector.tensor_copy(out=out, in_=in_)
-            else:
-                nc.scalar.copy(out=out, in_=in_)
+        def vector_copy(out, in_):
+            nc.vector.tensor_copy(out=out, in_=in_)
+
+        def scalar_copy(out, in_):
+            nc.scalar.copy(out=out, in_=in_)
+
+        def quantize(pair, first, width, values):
+            cols = slice(first, first + width)
+            nc.vector.quantize_mx(out=pair[0][:, cols].bitcast(FP8X4), scales=pair[1][:, cols], in_=values)
 
         def mx_group(bank, passes):
-            for i, (lhs, lcols, rhs, rscale) in enumerate(passes):
-                nc.tensor.matmul_mx(out=bank, lhsT=lhs[0][:, lcols].bitcast(FP8X4), lhsT_scale=lhs[1][:, lcols],
-                                    rhs=rhs, rhs_scale=rscale, start=(i == 0), stop=(i == len(passes) - 1))
+            for i, (pair, cols, codes, plane) in enumerate(passes):
+                nc.tensor.matmul_mx(out=bank, lhsT=pair[0][:, cols].bitcast(FP8X4), lhsT_scale=pair[1][:, cols],
+                                    rhs=codes, rhs_scale=plane, start=(i == 0), stop=(i == len(passes) - 1))
 
-        def step(name, eng):
-            kind = name[0]
-            if name == "Linv":
-                nc.scalar.dma_start(out=inv_sb[:], in_=inv.rearrange("(g p t) -> p g t", g=2, t=4))
-                nc.vector.memset(warm[:], 0.0)
-                nc.scalar.activation(out=warm_out[:], in_=warm[:], func=ACT.Relu)
-                make_identity(nc, ident[:])
-            elif name == "Ninv":
-                nc.vector.tensor_scalar(out=neg_inv[:], in0=inv_sb[:], scalar1=-1.0, scalar2=None, op0=ALU.mult)
-            elif name == "Lvs":
-                for q in range(4):
-                    nc.sync.dma_start(out=v_plane[32 * q:32 * q + 4, :, :].bitcast(I32),
-                                      in_=v_scales[:, 4 * q:4 * q + 4, :].rearrange("g r n -> r g n").bitcast(I32))
-            elif name == "Lv":
-                nc.sync.dma_start(out=v_codes[:].bitcast(I32), in_=v_words.rearrange("g p n -> p g n").bitcast(I32))
-            elif name[:2] == "Lg":
-                n = int(name[2])
-                nc.sync.dma_start(out=grad_sb[n][:], in_=grad[256 * n:256 * (n + 1), :].rearrange("(c p) d -> p c d", c=2))
-            elif kind == "L":
-                x, g, lo, hi = name[1], int(name[2]), int(name[3]), int(name[4])
-                rows = src[x][512 * g:512 * (g + 1), :].rearrange("(m t) k -> m t k", t=4)
-                nc.sync.dma_start(out=raw[x][g][:, lo:hi, :], in_=rows[:, lo:hi, :])
-            elif kind == "O":
-                zeros = stage.tile([P, 1024], BF16, name="zeros", tag="grouped", bufs=7, align_bytes=64)
-                nc.vector.memset(zeros[:].bitcast(I32), 0)
-                quantize(zero_mx[0], 0, 256, zeros[:])
-            elif kind == "M":
-                nc.vector.memset(v_plane[:].rearrange("p g n -> p (g n)").bitcast(I32), 0)
-            elif kind == "D":
-                width = 128 * int(name[1])
-                bank = new_bank(name)
-                for i in range(int(name[2])):
-                    mx_group(bank[:, 0:width], [(zero_mx[0], slice(0, P), zero_mx[0][0][:, 0:width].bitcast(FP8X4), zero_mx[0][1][:, 0:width])])
-            elif kind == "P":
-                x, n = name[1], int(name[2])
-                words = raw[x][n // 4][:, n % 4, :].bitcast(F32)
-                split = stage.tile([P, 512], F32, name="split", tag="split", bufs=5, align_bytes=64)
-                copy(eng, split[:].rearrange("r (g u p) -> r g u p", g=2, u=2), words.rearrange("r (g p u) -> r g u p", g=2, u=2))
-                live[name] = split
-            elif kind == "T":
-                x, n = name[1], int(name[2])
-                bank = new_bank(name)
-                for g in range(2):
-                    for u in range(2):
-                        if name[1:] in PERMUTED:
-                            words = live["P" + name[1:]][:, 256 * g + P * u:256 * g + P * (u + 1)]
-                        else:
-                            words = raw[x][n // 4][:, n % 4, :].bitcast(F32)[:, 256 * g + u:256 * (g + 1):2]
-                        nc.tensor.transpose(bank[:, 256 * g + P * u:256 * g + P * (u + 1)], words, ident[:])
-            elif kind == "E":
-                grouped = stage.tile([P, 1024], BF16, name="grouped", tag="grouped", bufs=7, align_bytes=64)
-                copy(eng, grouped[:].bitcast(F32).rearrange("p (g r u) -> p g r u", g=2, u=2),
-                     live["T" + name[1:]][:].rearrange("p (g u r) -> p g r u", g=2, u=2))
-                live[name] = grouped
-            elif kind == "Q":
-                x, n = name[1], int(name[2])
-                grouped = live["E" + name[1:]]
-                if x == "a":
-                    for g in range(2):
-                        quantize(a_mx[2 * (n // 4) + g], P * (n % 4), P, grouped[:, 512 * g:512 * (g + 1)])
-                else:
-                    quantize((b_mx if x == "b" else m_mx)[n], 0, 256, grouped[:])
-            elif kind == "g":
-                n, half = int(name[2]), int(name[3])
-                bank = new_bank("G" + name[1:3]) if half == 0 else live["G" + name[1:3]]
-                cols = slice(256 * half, 256 * (half + 1))
-                mx_group(bank[:, cols], [(b_mx[n], slice(P * c, P * (c + 1)), a_mx[c][0][:, cols].bitcast(FP8X4), a_mx[c][1][:, cols])
-                                         for c in range(2)])
-            elif kind == "G":
-                g, n = int(name[1]), int(name[2])
-                mx_group(new_bank(name)[:], [(b_mx[n], slice(P * c, P * (c + 1)), a_mx[2 * g + c][0][:].bitcast(FP8X4), a_mx[2 * g + c][1][:])
-                                             for c in range(2)])
-            elif kind == "R":
-                g, n = int(name[1]), int(name[2])
-                out = h_plain[2 * g + n // 4][:, n % 4, :].rearrange("p (u m e) -> p u m e", u=2, e=2)
-                in_ = live["G" + name[1:]][:].rearrange("p (u e m) -> p u m e", u=2, e=2)
-                factor = neg_inv[:, n // 4, n % 4:n % 4 + 1]
-                if eng == "S":
-                    nc.scalar.activation(out=out, in_=in_, func=ACT.Relu, scale=factor)
-                else:
-                    nc.vector.tensor_scalar(out=out, in0=in_, scalar1=factor, scalar2=0.0, op0=ALU.mult, op1=ALU.max)
-            elif kind == "I":
-                g, j, half = int(name[1]), int(name[2]), int(name[3])
-                grouped = stage.tile([P, 1024], BF16, name="grouped", tag="grouped", bufs=7, align_bytes=64)
-                plain = h_plain[2 * g + j][:].rearrange("p t (u m e) -> p u m e t", u=2, e=2)
-                copy(eng, grouped[:].rearrange("p (m u e t) -> p u m e t", u=2, e=2, t=4), plain[:, :, 64 * half:64 * (half + 1)])
-                live[name] = grouped
-            elif kind == "X":
-                g, j, half = int(name[1]), int(name[2]), int(name[3])
-                quantize(hj_mx[2 * g + j], 256 * half, 256, live["I" + name[1:]][:])
-            elif kind == "H":
-                g, j, half = int(name[1]), int(name[2]), int(name[3])
-                bank = new_bank(name)
-                for tt in range(2):
-                    words = h_plain[2 * g + j][:, 2 * half + tt, :].bitcast(F32)
-                    for u in range(2):
-                        nc.tensor.transpose(bank[:, 256 * tt + P * u:256 * tt + P * (u + 1)], words[:, P * u:P * (u + 1)], ident[:])
-            elif kind == "J":
-                g, j, half = int(name[1]), int(name[2]), int(name[3])
-                key = "wide%d%d" % (g, j)
-                if key not in live:
-                    live[key] = stage.tile([P, 2048], BF16, name="wide", tag="wide", bufs=3, align_bytes=64)
-                copy(eng, live[key][:, 1024 * half:1024 * (half + 1)].bitcast(F32).rearrange("p (g r u) -> p g r u", g=2, u=2),
-                     live["H" + name[1:]][:].rearrange("p (g u r) -> p g r u", g=2, u=2))
-            elif kind == "Y":
-                g, j = int(name[1]), int(name[2])
-                quantize(hi_mx[2 * g + j], 0, 512, live["wide%d%d" % (g, j)][:])
-            elif kind == "W":
-                n, q = int(name[1]), int(name[2])
-                cols = slice(P * (n % 4), P * (n % 4 + 1))
-                mx_group(new_bank(name)[:], [(hj_mx[2 * (n // 4) + j], cols, v_codes[:, j, 1024 * q:1024 * (q + 1)].bitcast(FP4X4),
-                                              v_plane[:, j, 512 * q:512 * (q + 1)]) for j in range(2)])
-            elif kind == "F":
-                n, q = int(name[1]), int(name[2])
-                key = "fixed%d" % n
-                if key not in live:
-                    live[key] = stage.tile([P, D], F32, name="fixed", tag="fixed", bufs=OUT_BUFS, align_bytes=64)
-                cols = slice(512 * q, 512 * (q + 1))
-                nc.vector.tensor_tensor(out=live[key][:, cols], in0=live["W" + name[1:]][:], in1=grad_sb[n // 2][:, n % 2, cols], op=ALU.add)
-            elif kind == "S":
-                n, lo, hi = int(name[1]), int(name[2]), int(name[3])
-                cols = slice(512 * lo, 512 * hi)
-                nc.sync.dma_start(out=out_0[P * n:P * (n + 1), cols], in_=live["fixed%d" % n][:, cols])
-            elif kind == "C":
-                r, j = int(name[1]), int(name[2])
-                mx_group(new_bank(name)[:], [(m_mx[r], slice(P * g, P * (g + 1)), hi_mx[2 * g + j][0][:].bitcast(FP8X4), hi_mx[2 * g + j][1][:])
-                                             for g in range(2)])
-            elif kind == "K":
-                r, j = int(name[1]), int(name[2])
-                key = "charge%d" % r
-                if key not in live:
-                    live[key] = keep.tile([P, N], F32, name=key, align_bytes=64)
-                out = live[key][:, 512 * j:512 * (j + 1)].rearrange("p (m t) -> p m t", t=4)
-                in_ = live["C" + name[1:]][:].rearrange("p (t m) -> p m t", t=4)
-                if eng == "S":
-                    nc.scalar.activation(out=out, in_=in_, func=ACT.Copy, scale=-1.0)
-                else:
-                    nc.vector.tensor_scalar(out=out, in0=in_, scalar1=-1.0, scalar2=None, op0=ALU.mult)
-            elif kind == "Z":
-                r, lo, hi = int(name[1]), int(name[2]), int(name[3])
-                rows = out_1.rearrange("(m t) n -> m t n", t=4)
-                nc.sync.dma_start(out=rows[:, r, 512 * lo:512 * hi], in_=live["charge%d" % r][:, 512 * lo:512 * hi])
+        def block(i):
+            return slice(P * i, P * (i + 1))
 
-        for item in ORDER:
-            parts = item.split(":")
-            step(parts[0], parts[1])
+        def transpose_four(bank, pairs):
+            for i in range(BANK // P):
+                nc.tensor.transpose(bank[:, block(i)], pairs[:, block(i)], ident[:])
+
+        def join_pairs(copy, out, bank):
+            copy(out.bitcast(F32).rearrange("p (s r u) -> p s r u", s=2, u=2),
+                 bank[:].rearrange("p (s u r) -> p s r u", s=2, u=2))
+
+        def keep_clock(key, count):
+            bank = new_bank(key)
+            for i in range(count):
+                mx_group(bank[:, 0:HALF], [(zero_mx, block(0), zero_mx[0][:].bitcast(FP8X4), zero_mx[1][:])])
+
+        def load_rows(x, g, first, last):
+            rows = source[x][GROUP * g:GROUP * (g + 1), :].rearrange("(p t) k -> p t k", t=PACK)
+            nc.sync.dma_start(out=raw[x][g][:, first:last, :], in_=rows[:, first:last, :])
+
+        def load_grad(i):
+            rows = grad[2 * P * i:2 * P * (i + 1), :].rearrange("(c p) d -> p c d", c=2)
+            nc.sync.dma_start(out=grad_sb[i][:], in_=rows)
+
+        def sort_pairs(x, n, copy):
+            pairs = raw[x][n // PACK][:, n % PACK, :].bitcast(F32)
+            tile = stage.tile([P, BANK], F32, name="sorted_pairs", tag="sorted_pairs", bufs=SORTED_BUFS, align_bytes=ALIGN)
+            copy(tile[:].rearrange("r (g u p) -> r g u p", g=PASSES, u=2), pairs.rearrange("r (g p u) -> r g u p", g=PASSES, u=2))
+            live["sorted", x, n] = tile
+
+        def turn(x, n):
+            transpose_four(new_bank(("turned", x, n)), live["sorted", x, n])
+
+        def gather(x, n, copy):
+            join_pairs(copy, new_grouped(("grouped", x, n))[:], live["turned", x, n])
+
+        def quantize_rows(x, n):
+            grouped = live["grouped", x, n]
+            if x == "a":
+                for c in range(PASSES):
+                    quantize(a_mx[PASSES * (n // PACK) + c], P * (n % PACK), P, grouped[:, GROUP * c:GROUP * (c + 1)])
+            else:
+                quantize((b_mx if x == "b" else mix_mx)[n], 0, PASSES * P, grouped[:])
+
+        def gram(gi, n):
+            moving = a_mx[PASSES * gi:PASSES * (gi + 1)]
+            mx_group(new_bank(("gram", gi, n))[:],
+                     [(b_mx[n], block(c), moving[c][0][:].bitcast(FP8X4), moving[c][1][:]) for c in range(PASSES)])
+
+        def conflict(gi, n):
+            nc.scalar.activation(out=h_plain[2 * gi + n // PACK][:, n % PACK, :].rearrange("p (u m e) -> p u m e", u=2, e=2),
+                                 in_=live["gram", gi, n][:].rearrange("p (u e m) -> p u m e", u=2, e=2),
+                                 func=ACT.Relu, scale=neg_inv[:, n // PACK, n % PACK:n % PACK + 1])
+
+        def interleave(gi, gj, half, copy):
+            plain = h_plain[2 * gi + gj][:].rearrange("p t (u m e) -> p u m e t", u=2, e=2)
+            quads = HALF // PACK
+            copy(new_grouped(("woven", gi, gj, half))[:].rearrange("p (m u e t) -> p u m e t", u=2, e=2, t=PACK),
+                 plain[:, :, quads * half:quads * (half + 1)])
+
+        def quantize_by_anchor(gi, gj, half):
+            quantize(h_by_anchor[2 * gi + gj], HALF * half, HALF, live["woven", gi, gj, half][:])
+
+        def turn_h(gi, gj, half):
+            pairs = h_plain[2 * gi + gj][:, 2 * half:2 * (half + 1), :].rearrange("p t c -> p (t c)").bitcast(F32)
+            transpose_four(new_bank(("turned_h", gi, gj, half)), pairs)
+
+        def gather_h(gi, gj, half):
+            if half == 0:
+                live["wide", gi, gj] = stage.tile([P, PACK * BANK], BF16, name="wide", tag="wide", bufs=WIDE_BUFS, align_bytes=ALIGN)
+            cols = slice(PACK * HALF * half, PACK * HALF * (half + 1))
+            join_pairs(scalar_copy, live["wide", gi, gj][:, cols], live["turned_h", gi, gj, half])
+
+        def quantize_by_task(gi, gj):
+            quantize(h_by_task[2 * gi + gj], 0, BANK, live["wide", gi, gj][:])
+
+        def store_fixed(n, first, last):
+            cols = slice(BANK * first, BANK * last)
+            nc.sync.dma_start(out=out_0[block(n), cols], in_=live["fixed", n][:, cols])
+
+        def fixed_rows(n, stores):
+            fixed = stage.tile([P, D], F32, name="fixed", tag="fixed", bufs=FIXED_BUFS, align_bytes=ALIGN)
+            live["fixed", n] = fixed
+            for q in range(D // BANK):
+                cols = slice(BANK * q, BANK * (q + 1))
+                bank = new_bank(("fixed", n, q))
+                mx_group(bank[:], [(h_by_anchor[2 * (n // PACK) + gj], block(n % PACK),
+                                    v_codes[:, gj, 2 * BANK * q:2 * BANK * (q + 1)].bitcast(FP4X4), v_plane[:, gj, cols])
+                                   for gj in range(PASSES)])
+                nc.vector.tensor_tensor(out=fixed[:, cols], in0=bank[:], in1=grad_sb[n // 2][:, n % 2, cols], op=ALU.add)
+                if q in stores:
+                    store_fixed(n, stores[q], q + 1)
+
+        def charge_bank(r, gj):
+            bank = new_bank(("charge", r, gj))
+            mx_group(bank[:], [(mix_mx[r], block(gi), h_by_task[2 * gi + gj][0][:].bitcast(FP8X4), h_by_task[2 * gi + gj][1][:])
+                               for gi in range(PASSES)])
+            return (charge_sb[r][:, BANK * gj:BANK * (gj + 1)].rearrange("r (p t) -> r p t", t=PACK),
+                    bank[:].rearrange("r (t p) -> r p t", t=PACK))
+
+        def store_charge(r, first, last):
+            cols = slice(BANK * first, BANK * last)
+            nc.sync.dma_start(out=out_1.rearrange("(p t) n -> p t n", t=PACK)[:, r, cols], in_=charge_sb[r][:, cols])
+
+        def charge_rows(r):
+            for gj in range(PASSES):
+                out, in_ = charge_bank(r, gj)
+                nc.scalar.activation(out=out, in_=in_, func=ACT.Copy, scale=-1.0)
+            store_charge(r, 0, PASSES)
+
+        nc.scalar.dma_start(out=inv_sb[:], in_=inv.rearrange("(g p t) -> p g t", g=PASSES, t=PACK))
+        zeros = new_grouped("zeros")
+        nc.vector.memset(zeros[:].bitcast(I32), 0)
+        nc.scalar.activation(out=table_out[:], in_=zeros[:, 0:8], func=ACT.Relu)
+        quantize(zero_mx, 0, HALF, zeros[:])
+        nc.vector.memset(ident[:], 0.0)
+        make_identity(nc, ident[:], nomemset=True)
+        nc.vector.memset(v_plane[:].rearrange("p g n -> p (g n)").bitcast(I32), 0)
+
+        for x in ("a", "b"):
+            for t in range(PACK):
+                load_rows(x, 0, t, t + 1)
+        load_rows("b", 1, 0, 2)
+        load_rows("b", 1, 2, PACK)
+        load_rows("a", 1, 0, PACK)
+        for quadrant in range(4):
+            rows = v_scales[:, 4 * quadrant:4 * (quadrant + 1), :].rearrange("g r n -> r g n")
+            nc.sync.dma_start(out=v_plane[32 * quadrant:32 * quadrant + 4, :, :].bitcast(I32), in_=rows.bitcast(I32))
+        nc.sync.dma_start(out=v_codes[:].bitcast(I32), in_=v_words.rearrange("g p n -> p g n").bitcast(I32))
+        load_grad(0)
+        load_grad(1)
+        load_rows("mix", 0, 0, PACK)
+        load_grad(2)
+        load_grad(3)
+
+        first_tiles = [(x, t) for x in ("a", "b") for t in range(PACK)]
+        lag = 3
+        clock_passes = {0: 6, 2: 4, 5: 4}
+        for s, (x, n) in enumerate(first_tiles):
+            if s in clock_passes:
+                keep_clock(("clock", s), clock_passes[s])
+            sort_pairs(x, n, vector_copy)
+            turn(x, n)
+            if s + 1 < len(first_tiles):
+                gather(x, n, scalar_copy)
+            if s >= lag:
+                quantize_rows(*first_tiles[s - lag])
+        nc.vector.tensor_scalar(out=neg_inv[:], in0=inv_sb[:], scalar1=-1.0, scalar2=None, op0=ALU.mult)
+        quantize_rows("b", 1)
+
+        for n in (0, 1):
+            gram(0, n)
+            conflict(0, n)
+        sort_pairs("b", 4, vector_copy)
+        sort_pairs("b", 5, vector_copy)
+        gather("b", 3, vector_copy)
+        sort_pairs("b", 6, vector_copy)
+        sort_pairs("b", 7, vector_copy)
+        for n in range(4, 8):
+            turn("b", n)
+        quantize_rows("b", 2)
+        quantize_rows("b", 3)
+        for n in (4, 6):
+            gather("b", n, scalar_copy)
+            gather("b", n + 1, vector_copy)
+            quantize_rows("b", n)
+            quantize_rows("b", n + 1)
+        for n in range(2, 8):
+            gram(0, n)
+            conflict(0, n)
+
+        for n in range(4, 8):
+            sort_pairs("a", n, vector_copy)
+        for n in range(4, 8):
+            turn("a", n)
+            gather("a", n, scalar_copy)
+        for gj in range(PASSES):
+            for half in range(2):
+                turn_h(0, gj, half)
+                gather_h(0, gj, half)
+        interleave(0, 0, 0, vector_copy)
+        quantize_by_anchor(0, 0, 0)
+        interleave(0, 1, 0, vector_copy)
+        quantize_rows("a", 4)
+        quantize_by_anchor(0, 1, 0)
+        for n in range(5, 8):
+            quantize_rows("a", n)
+        halves = {1: 0, 3: 2}
+        fixed_rows(0, halves)
+
+        for n in range(8):
+            gram(1, n)
+            conflict(1, n)
+        for gj in range(PASSES):
+            interleave(0, gj, 1, vector_copy)
+            quantize_by_task(0, gj)
+            quantize_by_anchor(0, gj, 1)
+        interleave(1, 0, 0, vector_copy)
+        fixed_rows(1, halves)
+
+        for n in range(3):
+            sort_pairs("mix", n, scalar_copy)
+        for gj in range(PASSES):
+            for half in range(2):
+                turn_h(1, gj, half)
+                gather_h(1, gj, half)
+            if gj == 0:
+                sort_pairs("mix", 3, scalar_copy)
+        interleave(1, 1, 0, vector_copy)
+        quantize_by_anchor(1, 0, 0)
+        quantize_by_anchor(1, 1, 0)
+        fixed_rows(2, halves)
+        for n in range(PACK):
+            turn("mix", n)
+            gather("mix", n, scalar_copy)
+        for gj in range(PASSES):
+            quantize_by_task(1, gj)
+            interleave(1, gj, 1, scalar_copy)
+        fixed_rows(3, halves)
+
+        for r in range(PACK - 1):
+            quantize_rows("mix", r)
+            if r == 1:
+                quantize_by_anchor(1, 0, 1)
+                quantize_by_anchor(1, 1, 1)
+            fixed_rows(PACK + r, halves)
+            charge_rows(r)
+
+        last = PACK - 1
+        quantize_rows("mix", last)
+        fixed_rows(PACK + last, {1: 0, 2: 2, 3: 3})
+        out, in_ = charge_bank(last, 0)
+        nc.scalar.activation(out=out, in_=in_, func=ACT.Copy, scale=-1.0)
+        store_charge(last, 0, 1)
+        out, in_ = charge_bank(last, 1)
+        nc.vector.tensor_scalar(out=out, in0=in_, scalar1=-1.0, scalar2=None, op0=ALU.mult)
+        store_charge(last, 1, PASSES)

from contextlib import ExitStack

import concourse.mybir as mybir
from concourse.masks import make_identity

M, N, K, D, R = 1024, 1024, 1024, 2048, 512
FLOPS = 2 * M * N * K + 2 * M * N * D + 2 * R * M * N

F32 = mybir.dt.float32
BF16 = mybir.dt.bfloat16
I32 = mybir.dt.int32
U32 = mybir.dt.uint32
U8 = mybir.dt.uint8
FP8X4 = mybir.dt.float8_e4m3fn_x4
FP4X4 = mybir.dt.float4_e2m1fn_x4
ACT = mybir.ActivationFunctionType
ALU = mybir.AluOpType

P = 128
PACK = 4
GROUP = P * PACK
PASSES = 2
BANK = 512
BANKS = 8
HALF = 256
ALIGN = 64

SORTED_BUFS = 5
GROUPED_BUFS = 7
WIDE_BUFS = 3
FIXED_BUFS = 4


def tile_conflict_gradient_surgery_s8_kernel(tc, a, b, inv, grad, v_words, v_scales, mix, out_0, out_1):
    nc = tc.nc
    with ExitStack() as ctx:
        keep = ctx.enter_context(tc.tile_pool(name="keep", bufs=1))
        stage = ctx.enter_context(tc.tile_pool(name="stage", bufs=1))
        psum = ctx.enter_context(tc.psum_pool(name="psum", bufs=1))
        ctx.enter_context(tc.manual_schedule())

        def kept(name, shape, dtype):
            return keep.tile(shape, dtype, name=name, align_bytes=ALIGN)

        def mx_tiles(name, count, width):
            return [(kept("%s_codes%d" % (name, i), [P, width], U32), kept("%s_plane%d" % (name, i), [P, width], U8))
                    for i in range(count)]

        source = {"a": a, "b": b, "mix": mix}
        raw = {x: [kept("%s_raw%d" % (x, g), [P, PACK, K], BF16) for g in range(source[x].shape[0] // GROUP)]
               for x in ("a", "b", "mix")}
        grad_sb = [kept("grad%d" % i, [P, 2, D], BF16) for i in range(M // (2 * P))]
        v_codes = kept("v_codes", [P, PASSES, 2 * D], U8)
        v_plane = kept("v_plane", [P, PASSES, D], U8)
        inv_sb = kept("inv_sb", [P, PASSES, PACK], BF16)
        neg_inv = kept("neg_inv", [P, PASSES, PACK], F32)
        ident = kept("ident", [P, P], F32)
        table_out = kept("table_out", [P, 8], F32)

        a_mx = mx_tiles("a", 2 * PASSES, BANK)
        b_mx = mx_tiles("b", N // P, PASSES * P)
        mix_mx = mx_tiles("mix", R // P, PASSES * P)
        h_by_anchor = mx_tiles("hj", 2 * PASSES, BANK)
        h_by_task = mx_tiles("hi", 2 * PASSES, BANK)
        h_plain = [kept("h_plain%d" % i, [P, PACK, BANK], BF16) for i in range(2 * PASSES)]
        zero_mx = mx_tiles("zero", 1, HALF)[0]
        charge_sb = [kept("charge%d" % r, [P, N], F32) for r in range(R // P)]

        live = {}
        opened = []

        def new_bank(key):
            tag = "bank%d" % (len(opened) % BANKS)
            opened.append(key)
            live[key] = psum.tile([P, BANK], F32, name=tag, tag=tag)
            return live[key]

        def new_grouped(key):
            live[key] = stage.tile([P, PACK * HALF], BF16, name="grouped", tag="grouped", bufs=GROUPED_BUFS, align_bytes=ALIGN)
            return live[key]

        def vector_copy(out, in_):
            nc.vector.tensor_copy(out=out, in_=in_)

        def scalar_copy(out, in_):
            nc.scalar.copy(out=out, in_=in_)

        def quantize(pair, first, width, values):
            cols = slice(first, first + width)
            nc.vector.quantize_mx(out=pair[0][:, cols].bitcast(FP8X4), scales=pair[1][:, cols], in_=values)

        def mx_group(bank, passes):
            for i, (pair, cols, codes, plane) in enumerate(passes):
                nc.tensor.matmul_mx(out=bank, lhsT=pair[0][:, cols].bitcast(FP8X4), lhsT_scale=pair[1][:, cols],
                                    rhs=codes, rhs_scale=plane, start=(i == 0), stop=(i == len(passes) - 1))

        def block(i):
            return slice(P * i, P * (i + 1))

        def transpose_four(bank, pairs):
            for i in range(BANK // P):
                nc.tensor.transpose(bank[:, block(i)], pairs[:, block(i)], ident[:])

        def join_pairs(copy, out, bank):
            copy(out.bitcast(F32).rearrange("p (s r u) -> p s r u", s=2, u=2),
                 bank[:].rearrange("p (s u r) -> p s r u", s=2, u=2))

        def keep_clock(key, count):
            bank = new_bank(key)
            for i in range(count):
                mx_group(bank[:, 0:HALF], [(zero_mx, block(0), zero_mx[0][:].bitcast(FP8X4), zero_mx[1][:])])

        def load_rows(x, g, first, last):
            rows = source[x][GROUP * g:GROUP * (g + 1), :].rearrange("(p t) k -> p t k", t=PACK)
            nc.sync.dma_start(out=raw[x][g][:, first:last, :], in_=rows[:, first:last, :])

        def load_grad(i):
            rows = grad[2 * P * i:2 * P * (i + 1), :].rearrange("(c p) d -> p c d", c=2)
            nc.sync.dma_start(out=grad_sb[i][:], in_=rows)

        def sort_pairs(x, n, copy):
            pairs = raw[x][n // PACK][:, n % PACK, :].bitcast(F32)
            tile = stage.tile([P, BANK], F32, name="sorted_pairs", tag="sorted_pairs", bufs=SORTED_BUFS, align_bytes=ALIGN)
            copy(tile[:].rearrange("r (g u p) -> r g u p", g=PASSES, u=2), pairs.rearrange("r (g p u) -> r g u p", g=PASSES, u=2))
            live["sorted", x, n] = tile

        def turn(x, n):
            transpose_four(new_bank(("turned", x, n)), live["sorted", x, n])

        def gather(x, n, copy):
            join_pairs(copy, new_grouped(("grouped", x, n))[:], live["turned", x, n])

        def quantize_rows(x, n):
            grouped = live["grouped", x, n]
            if x == "a":
                for c in range(PASSES):
                    quantize(a_mx[PASSES * (n // PACK) + c], P * (n % PACK), P, grouped[:, GROUP * c:GROUP * (c + 1)])
            else:
                quantize((b_mx if x == "b" else mix_mx)[n], 0, PASSES * P, grouped[:])

        def gram(gi, n):
            moving = a_mx[PASSES * gi:PASSES * (gi + 1)]
            mx_group(new_bank(("gram", gi, n))[:],
                     [(b_mx[n], block(c), moving[c][0][:].bitcast(FP8X4), moving[c][1][:]) for c in range(PASSES)])

        def conflict(gi, n):
            nc.scalar.activation(out=h_plain[2 * gi + n // PACK][:, n % PACK, :].rearrange("p (u m e) -> p u m e", u=2, e=2),
                                 in_=live["gram", gi, n][:].rearrange("p (u e m) -> p u m e", u=2, e=2),
                                 func=ACT.Relu, scale=neg_inv[:, n // PACK, n % PACK:n % PACK + 1])

        def interleave(gi, gj, half, copy):
            plain = h_plain[2 * gi + gj][:].rearrange("p t (u m e) -> p u m e t", u=2, e=2)
            quads = HALF // PACK
            copy(new_grouped(("woven", gi, gj, half))[:].rearrange("p (m u e t) -> p u m e t", u=2, e=2, t=PACK),
                 plain[:, :, quads * half:quads * (half + 1)])

        def quantize_by_anchor(gi, gj, half):
            quantize(h_by_anchor[2 * gi + gj], HALF * half, HALF, live["woven", gi, gj, half][:])

        def turn_h(gi, gj, half):
            pairs = h_plain[2 * gi + gj][:, 2 * half:2 * (half + 1), :].rearrange("p t c -> p (t c)").bitcast(F32)
            transpose_four(new_bank(("turned_h", gi, gj, half)), pairs)

        def gather_h(gi, gj, half):
            if half == 0:
                live["wide", gi, gj] = stage.tile([P, PACK * BANK], BF16, name="wide", tag="wide", bufs=WIDE_BUFS, align_bytes=ALIGN)
            cols = slice(PACK * HALF * half, PACK * HALF * (half + 1))
            join_pairs(scalar_copy, live["wide", gi, gj][:, cols], live["turned_h", gi, gj, half])

        def quantize_by_task(gi, gj):
            quantize(h_by_task[2 * gi + gj], 0, BANK, live["wide", gi, gj][:])

        def store_fixed(n, first, last):
            cols = slice(BANK * first, BANK * last)
            nc.sync.dma_start(out=out_0[block(n), cols], in_=live["fixed", n][:, cols])

        def fixed_rows(n, stores):
            fixed = stage.tile([P, D], F32, name="fixed", tag="fixed", bufs=FIXED_BUFS, align_bytes=ALIGN)
            live["fixed", n] = fixed
            for q in range(D // BANK):
                cols = slice(BANK * q, BANK * (q + 1))
                bank = new_bank(("fixed", n, q))
                mx_group(bank[:], [(h_by_anchor[2 * (n // PACK) + gj], block(n % PACK),
                                    v_codes[:, gj, 2 * BANK * q:2 * BANK * (q + 1)].bitcast(FP4X4), v_plane[:, gj, cols])
                                   for gj in range(PASSES)])
                nc.vector.tensor_tensor(out=fixed[:, cols], in0=bank[:], in1=grad_sb[n // 2][:, n % 2, cols], op=ALU.add)
                if q in stores:
                    store_fixed(n, stores[q], q + 1)

        def charge_bank(r, gj):
            bank = new_bank(("charge", r, gj))
            mx_group(bank[:], [(mix_mx[r], block(gi), h_by_task[2 * gi + gj][0][:].bitcast(FP8X4), h_by_task[2 * gi + gj][1][:])
                               for gi in range(PASSES)])
            return (charge_sb[r][:, BANK * gj:BANK * (gj + 1)].rearrange("r (p t) -> r p t", t=PACK),
                    bank[:].rearrange("r (t p) -> r p t", t=PACK))

        def store_charge(r, first, last):
            cols = slice(BANK * first, BANK * last)
            nc.sync.dma_start(out=out_1.rearrange("(p t) n -> p t n", t=PACK)[:, r, cols], in_=charge_sb[r][:, cols])

        def charge_rows(r):
            for gj in range(PASSES):
                out, in_ = charge_bank(r, gj)
                nc.scalar.activation(out=out, in_=in_, func=ACT.Copy, scale=-1.0)
            store_charge(r, 0, PASSES)

        nc.scalar.dma_start(out=inv_sb[:], in_=inv.rearrange("(g p t) -> p g t", g=PASSES, t=PACK))
        zeros = new_grouped("zeros")
        nc.vector.memset(zeros[:].bitcast(I32), 0)
        nc.scalar.activation(out=table_out[:], in_=zeros[:, 0:8], func=ACT.Relu)
        quantize(zero_mx, 0, HALF, zeros[:])
        nc.vector.memset(ident[:], 0.0)
        make_identity(nc, ident[:], nomemset=True)
        nc.vector.memset(v_plane[:].rearrange("p g n -> p (g n)").bitcast(I32), 0)

        for x in ("a", "b"):
            for t in range(PACK):
                load_rows(x, 0, t, t + 1)
        load_rows("b", 1, 0, 2)
        load_rows("b", 1, 2, PACK)
        load_rows("a", 1, 0, PACK)
        for quadrant in range(4):
            rows = v_scales[:, 4 * quadrant:4 * (quadrant + 1), :].rearrange("g r n -> r g n")
            nc.sync.dma_start(out=v_plane[32 * quadrant:32 * quadrant + 4, :, :].bitcast(I32), in_=rows.bitcast(I32))
        nc.sync.dma_start(out=v_codes[:].bitcast(I32), in_=v_words.rearrange("g p n -> p g n").bitcast(I32))
        load_grad(0)
        load_grad(1)
        load_rows("mix", 0, 0, PACK)
        load_grad(2)
        load_grad(3)

        first_tiles = [(x, t) for x in ("a", "b") for t in range(PACK)]
        lag = 3
        clock_passes = {0: 6, 2: 4, 5: 4}
        for s, (x, n) in enumerate(first_tiles):
            if s in clock_passes:
                keep_clock(("clock", s), clock_passes[s])
            sort_pairs(x, n, vector_copy)
            turn(x, n)
            if s + 1 < len(first_tiles):
                gather(x, n, scalar_copy)
            if s >= lag:
                quantize_rows(*first_tiles[s - lag])
        nc.vector.tensor_scalar(out=neg_inv[:], in0=inv_sb[:], scalar1=-1.0, scalar2=None, op0=ALU.mult)
        quantize_rows("b", 1)

        for n in (0, 1):
            gram(0, n)
            conflict(0, n)
        sort_pairs("b", 4, vector_copy)
        sort_pairs("b", 5, vector_copy)
        gather("b", 3, vector_copy)
        sort_pairs("b", 6, vector_copy)
        sort_pairs("b", 7, vector_copy)
        for n in range(4, 8):
            turn("b", n)
        quantize_rows("b", 2)
        quantize_rows("b", 3)
        for n in (4, 6):
            gather("b", n, scalar_copy)
            gather("b", n + 1, vector_copy)
            quantize_rows("b", n)
            quantize_rows("b", n + 1)
        for n in range(2, 8):
            gram(0, n)
            conflict(0, n)

        for n in range(4, 8):
            sort_pairs("a", n, vector_copy)
        for n in range(4, 8):
            turn("a", n)
            gather("a", n, scalar_copy)
        for gj in range(PASSES):
            for half in range(2):
                turn_h(0, gj, half)
                gather_h(0, gj, half)
        interleave(0, 0, 0, vector_copy)
        quantize_by_anchor(0, 0, 0)
        interleave(0, 1, 0, vector_copy)
        quantize_rows("a", 4)
        quantize_by_anchor(0, 1, 0)
        for n in range(5, 8):
            quantize_rows("a", n)
        halves = {1: 0, 3: 2}
        fixed_rows(0, halves)

        for n in range(8):
            gram(1, n)
            conflict(1, n)
        for gj in range(PASSES):
            interleave(0, gj, 1, vector_copy)
            quantize_by_task(0, gj)
            quantize_by_anchor(0, gj, 1)
        interleave(1, 0, 0, vector_copy)
        fixed_rows(1, halves)

        for n in range(3):
            sort_pairs("mix", n, scalar_copy)
        for gj in range(PASSES):
            for half in range(2):
                turn_h(1, gj, half)
                gather_h(1, gj, half)
            if gj == 0:
                sort_pairs("mix", 3, scalar_copy)
        interleave(1, 1, 0, vector_copy)
        quantize_by_anchor(1, 0, 0)
        quantize_by_anchor(1, 1, 0)
        fixed_rows(2, halves)
        for n in range(PACK):
            turn("mix", n)
            gather("mix", n, scalar_copy)
        for gj in range(PASSES):
            quantize_by_task(1, gj)
            interleave(1, gj, 1, scalar_copy)
        fixed_rows(3, halves)

        for r in range(PACK - 1):
            quantize_rows("mix", r)
            if r == 1:
                quantize_by_anchor(1, 0, 1)
                quantize_by_anchor(1, 1, 1)
            fixed_rows(PACK + r, halves)
            charge_rows(r)

        last = PACK - 1
        quantize_rows("mix", last)
        fixed_rows(PACK + last, {1: 0, 2: 2, 3: 3})
        out, in_ = charge_bank(last, 0)
        nc.scalar.activation(out=out, in_=in_, func=ACT.Copy, scale=-1.0)
        store_charge(last, 0, 1)
        out, in_ = charge_bank(last, 1)
        nc.vector.tensor_scalar(out=out, in0=in_, scalar1=-1.0, scalar2=None, op0=ALU.mult)
        store_charge(last, 1, PASSES)
